import numpy as np
import ml_dtypes


def mxq(x, axis, fmt="e4m3"):
    dtype, down = {"e4m3": (ml_dtypes.float8_e4m3fn, 7), "e5m2": (ml_dtypes.float8_e5m2, 14)}[fmt]
    v = np.moveaxis(np.asarray(x, np.float32).astype(ml_dtypes.bfloat16).astype(np.float64), axis, -1)
    blocks = v.reshape(v.shape[:-1] + (-1, 32))
    amax = np.abs(blocks).max(-1, keepdims=True)
    byte = np.maximum(np.where(amax > 0, np.frexp(amax)[1] - 1 + 127, 0) - down, 1)
    scale = np.exp2(byte - 127.0)
    codes = (blocks / scale).astype(np.float32).astype(dtype).astype(np.float64)
    return np.moveaxis((codes * scale).reshape(v.shape), -1, axis)


WIDE = False


def mx_kscale(k):
    if not WIDE:
        return np.ones(k)
    levels = np.array([10, -10, 5, -5, 0])
    if k % 512:
        return np.exp2(np.random.permutation(np.resize(levels, k // 32))).repeat(32)
    a = np.empty((k // 512, 16))
    for p in range(k // 512):
        a[p, :8] = np.random.permutation(np.resize(levels, 8))
        for g in range(8):
            far = levels[np.abs(levels - a[p, g]) >= 10]
            a[p, g + 8] = far[np.random.randint(len(far))]
    return np.exp2(a.ravel()).repeat(32)


def f64(x):
    return np.asarray(x).astype(np.float64)


def striped8(idx):
    return np.asarray(idx).reshape(8, -1, 16).transpose(0, 2, 1).reshape(128, -1).astype(np.uint16)


def unstriped8(offs):
    return offs.reshape(8, 16, -1).transpose(0, 2, 1).reshape(8, -1).astype(np.int64)


def pick8(x, idx, run):
    r = np.arange(len(x))
    return x[r[:, None], idx[r % (8 * run) // run]]


E2M1 = np.array([0.0, 0.5, 1.0, 1.5, 2.0, 3.0, 4.0, 6.0, -0.0, -0.5, -1.0, -1.5, -2.0, -3.0, -4.0, -6.0])


def pack_weight(w, fmt):
    k, n = w.shape
    w = f64(np.asarray(w, np.float32).astype(ml_dtypes.bfloat16)).reshape(k // 32, 32, n)
    amax = np.abs(w).max(1)
    if fmt == "e4m3":
        byte = np.frexp(amax)[1] - 1 + 127 - 7
    else:
        mant, ex = np.frexp(amax / 6.0)
        byte = np.where(mant > 0.5, ex, ex - 1) + 127
    byte = np.clip(np.where(amax > 0, byte, 1), 1, 254)
    scaled = (w * np.exp2(127.0 - byte)[:, None, :]).reshape(k, n).astype(np.float32)
    by_word = np.ascontiguousarray(scaled.reshape(k // 512, 128, 4, n).transpose(0, 1, 3, 2))
    if fmt == "e4m3":
        words = by_word.astype(ml_dtypes.float8_e4m3fn).view(np.uint8)
    else:
        c = by_word.astype(ml_dtypes.float4_e2m1fn).view(np.uint8) & 0xF
        words = (c[..., 0::2] | (c[..., 1::2] << 4)).reshape(k // 512, 128, 2 * n)
    return np.ascontiguousarray(words), np.ascontiguousarray(byte.astype(np.uint8).reshape(k // 512, 16, n))


def unpack_weight(words, scales, fmt):
    g, _, n = scales.shape
    words = np.ascontiguousarray(words).reshape(g, 128, n, -1)
    if fmt == "e4m3":
        vals = words.view(ml_dtypes.float8_e4m3fn).astype(np.float64)
    else:
        nib = np.empty((g, 128, n, 4), np.uint8)
        nib[..., 0::2] = words & 0xF
        nib[..., 1::2] = words >> 4
        vals = E2M1[nib]
    vals = vals * np.repeat(np.exp2(scales.astype(np.float64) - 127.0), 8, axis=1)[..., None]
    return vals.transpose(0, 1, 3, 2).reshape(g * 512, n)


D, T, I, Q, E = 512, 1024, 512, 512, 256


def setup_inputs():
    n = np.random.standard_normal
    idx = np.stack([np.random.permutation(T)[:I] for _ in range(8)])
    idx2 = np.stack([np.random.permutation(T)[:I] for _ in range(8)])
    idx3 = np.stack([np.random.permutation(T)[:I] for _ in range(8)])
    idx4 = np.stack([np.random.permutation(T)[:I] for _ in range(8)])
    idx5 = np.stack([np.random.permutation(T)[:I] for _ in range(8)])
    fd = mx_kscale(D)
    fq = mx_kscale(Q)
    cachep = pack_weight(n((D, T)) / fd[:, None], "e2m1")
    mixp = pack_weight(n((Q, E)) * 1.0 / np.sqrt(Q) / fq[:, None], "e4m3")
    return {
        "query": (n((D, Q)) * 1.0 / np.sqrt(D) * fd[:, None]).astype(np.float32),
        "cache_words": cachep[0],
        "cache_scales": cachep[1],
        "rowf": (np.random.uniform(0.5, 2.0, (Q, 1)) * fq[:, None]).astype(np.float32),
        "mix_words": mixp[0],
        "mix_scales": mixp[1],
        "offs": striped8(idx),
        "offs2": striped8(idx2),
        "offs3": striped8(idx3),
        "offs4": striped8(idx4),
        "offs5": striped8(idx5),
    }


def reference(query, cache_words, cache_scales, rowf, mix_words, mix_scales, offs, offs2, offs3, offs4, offs5):
    idx = unstriped8(offs)
    idx2 = unstriped8(offs2)
    idx3 = unstriped8(offs3)
    idx4 = unstriped8(offs4)
    idx5 = unstriped8(offs5)
    cacheu = unpack_weight(cache_words, cache_scales, "e2m1")
    mixu = unpack_weight(mix_words, mix_scales, "e4m3")
    queryq = mxq(f64(query), 0, "e4m3")
    a = queryq.T @ cacheu
    a1 = np.pad(a, ((0, 0), (1, 0)))[:, :T]
    w = np.maximum(pick8(a1, idx, 64), pick8(a, idx2, 64))
    f1 = np.zeros((Q, T))
    f1[np.arange(Q)[:, None], idx3[np.arange(Q) % 512 // 64]] = w
    f2 = np.zeros((Q, T))
    f2[np.arange(Q)[:, None], idx4[np.arange(Q) % 512 // 64]] = pick8(a1, idx, 64)
    c1 = a - f1
    c2 = np.maximum(c1, f2)
    g = pick8(c2, idx5, 64) + pick8(a1, idx2, 64)
    gw = g * f64(rowf)
    gwq = mxq(gw, 0, "e4m3")
    y = mixu.T @ gwq
    return y

@@ -1,0 +1,250 @@
+from contextlib import ExitStack
+
+import concourse.mybir as mybir
+
+D, T, I, Q, E = 512, 1024, 512, 512, 256
+FLOPS = 2 * D * Q * T + 2 * Q * E * I
+
+F32 = mybir.dt.float32
+BF16 = mybir.dt.bfloat16
+I32 = mybir.dt.int32
+U32 = mybir.dt.uint32
+U16 = mybir.dt.uint16
+U8 = mybir.dt.uint8
+FP8X4 = mybir.dt.float8_e4m3fn_x4
+FP4X4 = mybir.dt.float4_e2m1fn_x4
+ALU = mybir.AluOpType
+COPY = mybir.ActivationFunctionType.Copy
+
+P = 128
+PACK = 4
+BANK = 512
+HALF = 256
+
+
+def tile_attend_nexttoken_one_mixed_kernel(
+    tc, query, cache_words, cache_scales, rowf, mix_words, mix_scales, offs, offs2, offs3, offs4, offs5, out
+):
+    nc = tc.nc
+    with ExitStack() as ctx:
+        keep = ctx.enter_context(tc.tile_pool(name="keep", bufs=1))
+        psum = ctx.enter_context(tc.psum_pool(name="psum", bufs=8))
+
+        def f32_tiles(name, width, count):
+            return [keep.tile([P, width], F32, name="%s%d" % (name, n)) for n in range(count)]
+
+        cs_stage = keep.tile([PACK, PACK, T], U8, name="cs_stage")
+        nc.sync.dma_start(
+            out=cs_stage[:].bitcast(I32), in_=cache_scales[0].rearrange("(g f) t -> f g t", f=PACK).bitcast(I32)
+        )
+        q_rows = query.rearrange("(p j) q -> p j q", j=PACK)
+        q_raw = []
+        for h in range(2):
+            raw = keep.tile([P, PACK, HALF], F32, name="q_raw%d" % h)
+            nc.sync.dma_start(out=raw[:], in_=q_rows[:, :, h * HALF : (h + 1) * HALF])
+            q_raw.append(raw)
+        cache_codes = keep.tile([P, 2 * T], U8, name="cache_codes", align_bytes=64)
+        nc.sync.dma_start(out=cache_codes[:].bitcast(I32), in_=cache_words[0].bitcast(I32))
+        lists = {}
+        for name, src in (("offs", offs), ("offs2", offs2), ("offs4", offs4), ("offs3", offs3), ("offs5", offs5)):
+            lists[name] = keep.tile([P, I // 16], U16, name=name + "_sb")
+            nc.sync.dma_start(lists[name][:], src)
+        factor = keep.tile([P, PACK], F32, name="factor")
+        nc.sync.dma_start(out=factor[:], in_=rowf.rearrange("(p r) o -> p (r o)", r=PACK))
+        mix_codes = keep.tile([P, PACK * E], U8, name="mix_codes", align_bytes=64)
+        nc.sync.dma_start(
+            out=mix_codes[:].bitcast(I32), in_=mix_words[0].rearrange("p e r -> p (e r)").bitcast(I32)
+        )
+
+        cache_plane = keep.tile([P, T], U8, name="cache_plane", align_bytes=64)
+        nc.vector.memset(cache_plane[:].bitcast(I32), 0)
+        mix_plane = keep.tile([P, E], U8, name="mix_plane", align_bytes=64)
+        nc.gpsimd.memset(mix_plane[:].bitcast(I32), 0)
+        for g in range(PACK):
+            nc.sync.dma_start(
+                out=mix_plane[32 * g : 32 * g + PACK, :].bitcast(I32),
+                in_=mix_scales[0, PACK * g : PACK * (g + 1), :].bitcast(I32),
+            )
+
+        f1 = f32_tiles("f1_", T, 2)
+        f2 = f32_tiles("f2_", T, 2)
+        nc.vector.memset(f2[0][:], 0.0)
+        nc.vector.memset(f1[0][:], 0.0)
+        nc.gpsimd.memset(f1[1][:], 0.0)
+        nc.gpsimd.memset(f2[1][:], 0.0)
+        a = f32_tiles("a_", T, PACK)
+        a1 = f32_tiles("a1_", T + 1, PACK)
+        nc.vector.memset(a1[0][:, 0:1], 0.0)
+        for r in range(1, PACK):
+            nc.gpsimd.memset(a1[r][:, 0:1], 0.0)
+
+        for g in range(PACK):
+            nc.vector.tensor_copy(
+                out=cache_plane[32 * g : 32 * g + PACK, :].bitcast(I32), in_=cs_stage[:, g, :].bitcast(I32)
+            )
+
+        q_first = keep.tile([P, P, PACK], BF16, name="q_first", align_bytes=64)
+        q_rest = keep.tile([P, PACK - 1, P, PACK], BF16, name="q_rest", align_bytes=64)
+        for h in range(2):
+            s_range = slice(h * 64, (h + 1) * 64)
+            dealt = q_raw[h][:].rearrange("p j (s r) -> p s j r", r=PACK)
+            nc.vector.tensor_copy(out=q_first[:, s_range, :], in_=dealt[:, :, :, 0])
+            nc.scalar.activation(
+                out=q_rest[:, :, s_range, :].rearrange("p r s j -> p s j r"), in_=dealt[:, :, :, 1:PACK], func=COPY
+            )
+        qc_first = keep.tile([P, P], U32, name="qc_first", align_bytes=64)
+        qs_first = keep.tile([P, P], U8, name="qs_first", align_bytes=64)
+        nc.vector.quantize_mx(
+            out=qc_first[:].bitcast(FP8X4), scales=qs_first[:], in_=q_first[:].rearrange("p s j -> p (s j)")
+        )
+        qc_rest = keep.tile([P, 3 * P], U32, name="qc_rest", align_bytes=64)
+        qs_rest = keep.tile([P, 3 * P], U8, name="qs_rest", align_bytes=64)
+
+        def scores(r):
+            if r == 0:
+                codes, plane = qc_first[:], qs_first[:]
+            else:
+                cols = slice((r - 1) * P, r * P)
+                codes, plane = qc_rest[:, cols], qs_rest[:, cols]
+            banks = []
+            for b in range(2):
+                bank = psum.tile([P, BANK], F32, name="bank", tag="bank")
+                nc.tensor.matmul_mx(
+                    out=bank[:],
+                    lhsT=codes.bitcast(FP8X4),
+                    lhsT_scale=plane,
+                    rhs=cache_codes[:, 2 * BANK * b : 2 * BANK * (b + 1)].bitcast(FP4X4),
+                    rhs_scale=cache_plane[:, BANK * b : BANK * (b + 1)],
+                    start=True,
+                    stop=True,
+                )
+                banks.append(bank)
+            return banks
+
+        picked1 = f32_tiles("picked1_", I, PACK)
+        picked2 = f32_tiles("picked2_", I, PACK)
+        fore2 = f32_tiles("fore2_", I, PACK)
+        w = f32_tiles("w_", I, PACK)
+        g = f32_tiles("g_", I, PACK)
+        c1 = f32_tiles("c1_", T, PACK)
+        c2 = f32_tiles("c2_", T, PACK)
+        gw = keep.tile([P, I, PACK], BF16, name="gw", align_bytes=64)
+
+        def unload(r, banks, first_copy):
+            first_copy(out=a1[r][:, 1 : BANK + 1], in_=banks[0][:])
+            nc.scalar.copy(out=a1[r][:, BANK + 1 : T + 1], in_=banks[1][:])
+            nc.sync.dma_start(out=a[r][:], in_=a1[r][:, 1 : T + 1])
+
+        def pick_fore(r):
+            nc.vector.tensor_copy(out=picked1[r][:], in_=a1[r][:].indirect(lists["offs"][:]))
+
+        def pick_fore2(r):
+            nc.vector.tensor_copy(out=fore2[r][:], in_=a1[r][:].indirect(lists["offs2"][:]))
+
+        def pick_score2(r):
+            nc.vector.tensor_copy(out=picked2[r][:], in_=a[r][:].indirect(lists["offs2"][:]))
+
+        def larger(r):
+            nc.vector.tensor_tensor(out=w[r][:], in0=picked1[r][:], in1=picked2[r][:], op=ALU.max)
+
+        def put_f1(r):
+            nc.scalar.activation(out=f1[r % 2][:].indirect(lists["offs3"][:]), in_=w[r][:], func=COPY)
+
+        def put_f2(r):
+            nc.scalar.activation(out=f2[r % 2][:].indirect(lists["offs4"][:]), in_=picked1[r][:], func=COPY)
+
+        def make_c1(r):
+            nc.vector.tensor_tensor(out=c1[r][:], in0=a[r][:], in1=f1[r % 2][:], op=ALU.subtract)
+
+        def make_c2(r):
+            nc.vector.tensor_tensor(out=c2[r][:], in0=c1[r][:], in1=f2[r % 2][:], op=ALU.max)
+
+        def result(r, lo, hi):
+            nc.vector.tensor_tensor(
+                out=g[r][:, lo:hi],
+                in0=c2[r][:].indirect(lists["offs5"][:, lo // 16 : hi // 16]),
+                in1=fore2[r][:, lo:hi],
+                op=ALU.add,
+            )
+
+        def weigh(r, lo, hi):
+            nc.vector.tensor_scalar(
+                out=gw[:, lo:hi, r], in0=g[r][:, lo:hi], scalar1=factor[:, r : r + 1], scalar2=None, op0=ALU.mult
+            )
+
+        banks0 = scores(0)
+        nc.vector.quantize_mx(
+            out=qc_rest[:].bitcast(FP8X4), scales=qs_rest[:], in_=q_rest[:].rearrange("p r s j -> p (r s j)")
+        )
+        unload(0, banks0, nc.vector.tensor_copy)
+        later = [None] + [scores(r) for r in range(1, PACK)]
+        pick_fore(0)
+        unload(1, later[1], nc.scalar.copy)
+        put_f2(0)
+        pick_fore2(0)
+        pick_fore(1)
+        unload(2, later[2], nc.scalar.copy)
+        unload(3, later[3], nc.scalar.copy)
+        pick_score2(0)
+        pick_score2(1)
+        larger(0)
+        put_f1(0)
+        larger(1)
+        put_f1(1)
+        put_f2(1)
+        pick_fore2(1)
+        pick_fore(2)
+        pick_score2(2)
+        make_c1(0)
+        larger(2)
+        put_f1(2)
+        make_c2(0)
+        put_f2(2)
+        pick_fore(3)
+        result(0, 0, I)
+        pick_score2(3)
+        weigh(0, 0, I)
+        make_c1(1)
+        larger(3)
+        put_f1(3)
+        make_c2(1)
+        put_f2(3)
+        pick_fore2(2)
+        result(1, 0, I)
+        make_c1(2)
+        weigh(1, 0, I)
+        make_c2(2)
+        result(2, 0, I)
+        make_c1(3)
+        weigh(2, 0, I)
+        nc.scalar.activation(out=fore2[3][:], in_=a1[3][:].indirect(lists["offs2"][:]), func=COPY)
+        make_c2(3)
+        for h in range(2):
+            result(3, h * HALF, (h + 1) * HALF)
+        for h in range(2):
+            weigh(3, h * HALF, (h + 1) * HALF)
+
+        out_rows = out.rearrange("(b p) i -> p b i", p=P)
+        for h in range(2):
+            gc = keep.tile([P, HALF], U32, name="gc%d" % h, align_bytes=64)
+            gs = keep.tile([P, HALF], U8, name="gs%d" % h, align_bytes=64)
+            nc.vector.quantize_mx(
+                out=gc[:].bitcast(FP8X4), scales=gs[:], in_=gw[:, h * HALF : (h + 1) * HALF, :].rearrange("p i r -> p (i r)")
+            )
+            staged = keep.tile([P, 2, HALF], F32, name="staged%d" % h)
+            for b in range(2):
+                bank = psum.tile([P, BANK], F32, name="bank", tag="bank")
+                nc.tensor.matmul_mx(
+                    out=bank[:, 0:HALF],
+                    lhsT=mix_codes[:, PACK * P * b : PACK * P * (b + 1)].bitcast(FP8X4),
+                    lhsT_scale=mix_plane[:, P * b : P * (b + 1)],
+                    rhs=gc[:].bitcast(FP8X4),
+                    rhs_scale=gs[:],
+                    start=True,
+                    stop=True,
+                )
+                if h == 1 and b == 0:
+                    nc.vector.tensor_copy(out=staged[:, b, :], in_=bank[:, 0:HALF])
+                else:
+                    nc.scalar.copy(out=staged[:, b, :], in_=bank[:, 0:HALF])
+            nc.sync.dma_start(out=out_rows[:, :, h * HALF : (h + 1) * HALF], in_=staged[:])

@@ -67,15 +67,17 @@ def tile_attend_nexttoken_one_mixed_kernel(
             )
 
         f1 = f32_tiles("f1_", T, 2)
-        f2 = f32_tiles("f2_", T, 2)
-        nc.vector.memset(f2[0][:], 0.0)
+        f1 = [f1[0], f1[1], f1[0], f1[0]]
+        f2_even = keep.tile([P, T], F32, name="f2_even")
+        f2 = {0: f2_even, 2: f2_even}
+        nc.vector.memset(f2_even[:], 0.0)
         nc.vector.memset(f1[0][:], 0.0)
         nc.gpsimd.memset(f1[1][:], 0.0)
-        nc.gpsimd.memset(f2[1][:], 0.0)
         a = f32_tiles("a_", T, PACK)
         a1 = f32_tiles("a1_", T + 1, PACK)
         nc.vector.memset(a1[0][:, 0:1], 0.0)
-        for r in range(1, PACK):
+        nc.vector.memset(a1[2][:, 0:1], 0.0)
+        for r in (1, 3):
             nc.gpsimd.memset(a1[r][:, 0:1], 0.0)
 
         for g in range(PACK):
@@ -121,43 +123,46 @@ def tile_attend_nexttoken_one_mixed_kernel(
                 banks.append(bank)
             return banks
 
-        picked1 = f32_tiles("picked1_", I, PACK)
-        picked2 = f32_tiles("picked2_", I, PACK)
-        fore2 = f32_tiles("fore2_", I, PACK)
-        w = f32_tiles("w_", I, PACK)
+        arena = f32_tiles("arena_", T + I, PACK - 1)
+        own = f32_tiles("own_", I, 3)
+        c1_last = keep.tile([P, T], F32, name="c1_last")
+        c1 = [arena[r][:, 0:T] for r in range(PACK - 1)] + [c1_last[:]]
+        picked2 = [own[0][:]] + [arena[r][:, T - HALF : T + HALF] for r in range(PACK - 1)]
+        picked1 = [own[1][:], own[2][:], arena[0][:, T : T + I], arena[1][:, T : T + I]]
+        fore2 = [picked2[0], arena[0][:, 0:I], arena[0][:, I:T], picked1[3]]
+        w = [keep.tile([P, I], F32, name="w_%d" % r, tag="shared" if r == 1 else "w_%d" % r) for r in range(PACK)]
         g = f32_tiles("g_", I, PACK)
-        c1 = f32_tiles("c1_", T, PACK)
         c2 = f32_tiles("c2_", T, PACK)
         gw = keep.tile([P, I, PACK], BF16, name="gw", align_bytes=64)
 
-        def unload(r, banks, first_copy):
+        def unload(r, banks, first_copy, second_copy):
             first_copy(out=a1[r][:, 1 : BANK + 1], in_=banks[0][:])
-            nc.scalar.copy(out=a1[r][:, BANK + 1 : T + 1], in_=banks[1][:])
+            second_copy(out=a1[r][:, BANK + 1 : T + 1], in_=banks[1][:])
             nc.sync.dma_start(out=a[r][:], in_=a1[r][:, 1 : T + 1])
 
         def pick_fore(r):
-            nc.vector.tensor_copy(out=picked1[r][:], in_=a1[r][:].indirect(lists["offs"][:]))
+            nc.vector.tensor_copy(out=picked1[r], in_=a1[r][:].indirect(lists["offs"][:]))
 
         def pick_fore2(r):
-            nc.vector.tensor_copy(out=fore2[r][:], in_=a1[r][:].indirect(lists["offs2"][:]))
+            nc.vector.tensor_copy(out=fore2[r], in_=a1[r][:].indirect(lists["offs2"][:]))
 
         def pick_score2(r):
-            nc.vector.tensor_copy(out=picked2[r][:], in_=a[r][:].indirect(lists["offs2"][:]))
+            nc.vector.tensor_copy(out=picked2[r], in_=a[r][:].indirect(lists["offs2"][:]))
 
         def larger(r):
-            nc.vector.tensor_tensor(out=w[r][:], in0=picked1[r][:], in1=picked2[r][:], op=ALU.max)
+            nc.vector.tensor_tensor(out=w[r][:], in0=picked1[r], in1=picked2[r], op=ALU.max)
 
         def put_f1(r):
-            nc.scalar.activation(out=f1[r % 2][:].indirect(lists["offs3"][:]), in_=w[r][:], func=COPY)
+            nc.scalar.activation(out=f1[r][:].indirect(lists["offs3"][:]), in_=w[r][:], func=COPY)
 
         def put_f2(r):
-            nc.scalar.activation(out=f2[r % 2][:].indirect(lists["offs4"][:]), in_=picked1[r][:], func=COPY)
+            nc.scalar.activation(out=f2[r][:].indirect(lists["offs4"][:]), in_=picked1[r], func=COPY)
 
-        def make_c1(r):
-            nc.vector.tensor_tensor(out=c1[r][:], in0=a[r][:], in1=f1[r % 2][:], op=ALU.subtract)
+        def make_c1(r, engine):
+            engine.tensor_tensor(out=c1[r], in0=a[r][:], in1=f1[r][:], op=ALU.subtract)
 
         def make_c2(r):
-            nc.vector.tensor_tensor(out=c2[r][:], in0=c1[r][:], in1=f2[r % 2][:], op=ALU.max)
+            nc.vector.tensor_tensor(out=c2[r][:], in0=c1[r], in1=f2[r][:], op=ALU.max)
 
         def result(r, lo, hi):
             nc.vector.tensor_tensor(
@@ -176,53 +181,57 @@ def tile_attend_nexttoken_one_mixed_kernel(
         nc.vector.quantize_mx(
             out=qc_rest[:].bitcast(FP8X4), scales=qs_rest[:], in_=q_rest[:].rearrange("p r s j -> p (r s j)")
         )
-        unload(0, banks0, nc.vector.tensor_copy)
+        unload(0, banks0, nc.vector.tensor_copy, nc.scalar.copy)
         later = [None] + [scores(r) for r in range(1, PACK)]
         pick_fore(0)
-        unload(1, later[1], nc.scalar.copy)
+        unload(1, later[1], nc.scalar.copy, nc.scalar.copy)
         put_f2(0)
-        pick_fore2(0)
         pick_fore(1)
-        unload(2, later[2], nc.scalar.copy)
-        unload(3, later[3], nc.scalar.copy)
+        unload(2, later[2], nc.vector.tensor_copy, nc.vector.tensor_copy)
         pick_score2(0)
-        pick_score2(1)
         larger(0)
+        unload(3, later[3], nc.scalar.copy, nc.scalar.copy)
         put_f1(0)
+        pick_fore2(0)
+        pick_score2(1)
         larger(1)
         put_f1(1)
-        put_f2(1)
-        pick_fore2(1)
+        make_c1(0, nc.gpsimd)
         pick_fore(2)
         pick_score2(2)
-        make_c1(0)
         larger(2)
         put_f1(2)
+        make_c1(1, nc.gpsimd)
+        f2_odd = keep.tile([P, T], F32, name="f2_odd", tag="shared")
+        nc.gpsimd.memset(f2_odd[:], 0.0)
+        f2[1] = f2_odd
+        f2[3] = f2_odd
+        put_f2(1)
+        pick_fore(3)
+        pick_score2(3)
+        larger(3)
         make_c2(0)
         put_f2(2)
-        pick_fore(3)
-        result(0, 0, I)
-        pick_score2(3)
-        weigh(0, 0, I)
-        make_c1(1)
-        larger(3)
+        make_c1(2, nc.gpsimd)
         put_f1(3)
+        pick_fore2(1)
+        pick_fore2(2)
+        result(0, 0, I)
         make_c2(1)
         put_f2(3)
-        pick_fore2(2)
+        weigh(0, 0, I)
         result(1, 0, I)
-        make_c1(2)
-        weigh(1, 0, I)
         make_c2(2)
+        weigh(1, 0, I)
         result(2, 0, I)
-        make_c1(3)
+        make_c1(3, nc.vector)
         weigh(2, 0, I)
-        nc.scalar.activation(out=fore2[3][:], in_=a1[3][:].indirect(lists["offs2"][:]), func=COPY)
+        nc.scalar.activation(out=fore2[3], in_=a1[3][:].indirect(lists["offs2"][:]), func=COPY)
         make_c2(3)
         for h in range(2):
             result(3, h * HALF, (h + 1) * HALF)
-        for h in range(2):
-            weigh(3, h * HALF, (h + 1) * HALF)
+        nc.scalar.activation(out=gw[:, 0:HALF, 3], in_=g[3][:, 0:HALF], func=COPY, scale=factor[:, 3:4])
+        weigh(3, HALF, I)
 
         out_rows = out.rearrange("(b p) i -> p b i", p=P)
         for h in range(2):

@@ -33,10 +33,12 @@ def tile_attend_nexttoken_one_mixed_kernel(
         def f32_tiles(name, width, count):
             return [keep.tile([P, width], F32, name="%s%d" % (name, n)) for n in range(count)]
 
-        cs_stage = keep.tile([PACK, PACK, T], U8, name="cs_stage")
-        nc.sync.dma_start(
-            out=cs_stage[:].bitcast(I32), in_=cache_scales[0].rearrange("(g f) t -> f g t", f=PACK).bitcast(I32)
-        )
+        cs_stage = keep.tile([P, 2, T], U8, name="cs_stage")
+        scale_rows = cache_scales[0].rearrange("(g f) t -> f g t", f=PACK)
+        for u in range(2):
+            nc.sync.dma_start(
+                out=cs_stage[64 * u : 64 * u + PACK].bitcast(I32), in_=scale_rows[:, 2 * u : 2 * u + 2, :].bitcast(I32)
+            )
         q_rows = query.rearrange("(p j) q -> p j q", j=PACK)
         q_raw = []
         for h in range(2):
@@ -73,7 +75,7 @@ def tile_attend_nexttoken_one_mixed_kernel(
         nc.vector.memset(f2_even[:], 0.0)
         nc.vector.memset(f1[0][:], 0.0)
         nc.gpsimd.memset(f1[1][:], 0.0)
-        a = f32_tiles("a_", T, PACK)
+        a = [keep.tile([P, T], F32, name="a_%d" % r, tag="shared" if r == 0 else "a_%d" % r) for r in range(PACK)]
         a1 = f32_tiles("a1_", T + 1, PACK)
         nc.vector.memset(a1[0][:, 0:1], 0.0)
         nc.vector.memset(a1[2][:, 0:1], 0.0)
@@ -82,7 +84,7 @@ def tile_attend_nexttoken_one_mixed_kernel(
 
         for g in range(PACK):
             nc.vector.tensor_copy(
-                out=cache_plane[32 * g : 32 * g + PACK, :].bitcast(I32), in_=cs_stage[:, g, :].bitcast(I32)
+                out=cache_plane[32 * g : 32 * g + PACK, :].bitcast(I32), in_=cs_stage[64 * (g // 2) : 64 * (g // 2) + PACK, g % 2, :].bitcast(I32)
             )
 
         q_first = keep.tile([P, P, PACK], BF16, name="q_first", align_bytes=64)
@@ -92,52 +94,62 @@ def tile_attend_nexttoken_one_mixed_kernel(
             dealt = q_raw[h][:].rearrange("p j (s r) -> p s j r", r=PACK)
             nc.vector.tensor_copy(out=q_first[:, s_range, :], in_=dealt[:, :, :, 0])
             nc.scalar.activation(
-                out=q_rest[:, :, s_range, :].rearrange("p r s j -> p s j r"), in_=dealt[:, :, :, 1:PACK], func=COPY
+                out=q_rest[:, 0:2, s_range, :].rearrange("p r s j -> p s r j"),
+                in_=dealt[:, :, :, 1:3].rearrange("p s j r -> p s r j"),
+                func=COPY,
             )
         qc_first = keep.tile([P, P], U32, name="qc_first", align_bytes=64)
         qs_first = keep.tile([P, P], U8, name="qs_first", align_bytes=64)
         nc.vector.quantize_mx(
             out=qc_first[:].bitcast(FP8X4), scales=qs_first[:], in_=q_first[:].rearrange("p s j -> p (s j)")
         )
+        for h in range(2):
+            dealt = q_raw[h][:].rearrange("p j (s r) -> p s j r", r=PACK)
+            nc.vector.tensor_copy(out=q_rest[:, 2, h * 64 : (h + 1) * 64, :], in_=dealt[:, :, :, 3])
         qc_rest = keep.tile([P, 3 * P], U32, name="qc_rest", align_bytes=64)
         qs_rest = keep.tile([P, 3 * P], U8, name="qs_rest", align_bytes=64)
 
-        def scores(r):
+        def scores(r, width):
             if r == 0:
                 codes, plane = qc_first[:], qs_first[:]
             else:
                 cols = slice((r - 1) * P, r * P)
                 codes, plane = qc_rest[:, cols], qs_rest[:, cols]
             banks = []
-            for b in range(2):
+            for b in range(T // width):
                 bank = psum.tile([P, BANK], F32, name="bank", tag="bank")
                 nc.tensor.matmul_mx(
-                    out=bank[:],
+                    out=bank[:, 0:width],
                     lhsT=codes.bitcast(FP8X4),
                     lhsT_scale=plane,
-                    rhs=cache_codes[:, 2 * BANK * b : 2 * BANK * (b + 1)].bitcast(FP4X4),
-                    rhs_scale=cache_plane[:, BANK * b : BANK * (b + 1)],
+                    rhs=cache_codes[:, 2 * width * b : 2 * width * (b + 1)].bitcast(FP4X4),
+                    rhs_scale=cache_plane[:, width * b : width * (b + 1)],
                     start=True,
                     stop=True,
                 )
-                banks.append(bank)
+                banks.append(bank[:, 0:width])
             return banks
 
-        arena = f32_tiles("arena_", T + I, PACK - 1)
-        own = f32_tiles("own_", I, 3)
-        c1_last = keep.tile([P, T], F32, name="c1_last")
-        c1 = [arena[r][:, 0:T] for r in range(PACK - 1)] + [c1_last[:]]
-        picked2 = [own[0][:]] + [arena[r][:, T - HALF : T + HALF] for r in range(PACK - 1)]
-        picked1 = [own[1][:], own[2][:], arena[0][:, T : T + I], arena[1][:, T : T + I]]
-        fore2 = [picked2[0], arena[0][:, 0:I], arena[0][:, I:T], picked1[3]]
-        w = [keep.tile([P, I], F32, name="w_%d" % r, tag="shared" if r == 1 else "w_%d" % r) for r in range(PACK)]
+        strip = keep.tile([P, 23 * P], F32, name="strip")
+
+        def piece(start, width):
+            return strip[:, start * P : start * P + width]
+
+        own = f32_tiles("own_", I, 2)
+        c1_own = f32_tiles("c1_", T, 2)
+        w = f32_tiles("w_", I, PACK)
+        c1 = [piece(0, T), c1_own[0][:], piece(15, T), c1_own[1][:]]
+        picked2 = [piece(7, I), piece(7, I), piece(10, I), piece(12, I)]
+        picked1 = [own[0][:], own[1][:], own[0][:], piece(8, I)]
+        fore2 = [w[0][:], piece(0, I), piece(4, I), picked1[3]]
         g = f32_tiles("g_", I, PACK)
         c2 = f32_tiles("c2_", T, PACK)
         gw = keep.tile([P, I, PACK], BF16, name="gw", align_bytes=64)
 
         def unload(r, banks, first_copy, second_copy):
-            first_copy(out=a1[r][:, 1 : BANK + 1], in_=banks[0][:])
-            second_copy(out=a1[r][:, BANK + 1 : T + 1], in_=banks[1][:])
+            width = T // len(banks)
+            for b, bank in enumerate(banks):
+                (first_copy, second_copy)[b % 2](out=a1[r][:, 1 + b * width : 1 + (b + 1) * width], in_=bank)
             nc.sync.dma_start(out=a[r][:], in_=a1[r][:, 1 : T + 1])
 
         def pick_fore(r):
@@ -177,40 +189,40 @@ def tile_attend_nexttoken_one_mixed_kernel(
                 out=gw[:, lo:hi, r], in0=g[r][:, lo:hi], scalar1=factor[:, r : r + 1], scalar2=None, op0=ALU.mult
             )
 
-        banks0 = scores(0)
+        banks0 = scores(0, HALF)
         nc.vector.quantize_mx(
             out=qc_rest[:].bitcast(FP8X4), scales=qs_rest[:], in_=q_rest[:].rearrange("p r s j -> p (r s j)")
         )
         unload(0, banks0, nc.vector.tensor_copy, nc.scalar.copy)
-        later = [None] + [scores(r) for r in range(1, PACK)]
+        later = [None] + [scores(r, BANK) for r in range(1, PACK)]
         pick_fore(0)
         unload(1, later[1], nc.scalar.copy, nc.scalar.copy)
         put_f2(0)
         pick_fore(1)
-        unload(2, later[2], nc.vector.tensor_copy, nc.vector.tensor_copy)
         pick_score2(0)
         larger(0)
+        unload(2, later[2], nc.vector.tensor_copy, nc.vector.tensor_copy)
         unload(3, later[3], nc.scalar.copy, nc.scalar.copy)
         put_f1(0)
-        pick_fore2(0)
         pick_score2(1)
+        pick_fore(2)
         larger(1)
         put_f1(1)
         make_c1(0, nc.gpsimd)
-        pick_fore(2)
-        pick_score2(2)
-        larger(2)
-        put_f1(2)
-        make_c1(1, nc.gpsimd)
         f2_odd = keep.tile([P, T], F32, name="f2_odd", tag="shared")
         nc.gpsimd.memset(f2_odd[:], 0.0)
         f2[1] = f2_odd
         f2[3] = f2_odd
+        pick_score2(2)
+        pick_fore2(0)
+        larger(2)
+        put_f1(2)
+        make_c1(1, nc.gpsimd)
         put_f2(1)
-        pick_fore(3)
         pick_score2(3)
-        larger(3)
+        pick_fore(3)
         make_c2(0)
+        larger(3)
         put_f2(2)
         make_c1(2, nc.gpsimd)
         put_f1(3)
@@ -230,8 +242,8 @@ def tile_attend_nexttoken_one_mixed_kernel(
         make_c2(3)
         for h in range(2):
             result(3, h * HALF, (h + 1) * HALF)
-        nc.scalar.activation(out=gw[:, 0:HALF, 3], in_=g[3][:, 0:HALF], func=COPY, scale=factor[:, 3:4])
-        weigh(3, HALF, I)
+        for h in range(2):
+            weigh(3, h * HALF, (h + 1) * HALF)
 
         out_rows = out.rearrange("(b p) i -> p b i", p=P)
         for h in range(2):
@@ -256,4 +268,8 @@ def tile_attend_nexttoken_one_mixed_kernel(
                     nc.vector.tensor_copy(out=staged[:, b, :], in_=bank[:, 0:HALF])
                 else:
                     nc.scalar.copy(out=staged[:, b, :], in_=bank[:, 0:HALF])
-            nc.sync.dma_start(out=out_rows[:, :, h * HALF : (h + 1) * HALF], in_=staged[:])
+            if h == 0:
+                nc.sync.dma_start(out=out_rows[:, :, 0:HALF], in_=staged[:])
+            else:
+                nc.sync.dma_start(out=out_rows[:, 0, HALF:I], in_=staged[:, 0, :])
+                nc.scalar.dma_start(out=out_rows[:, 1, HALF:I], in_=staged[:, 1, :])

@@ -18,8 +18,21 @@ COPY = mybir.ActivationFunctionType.Copy
 
 P = 128
 PACK = 4
+QUADRANT = 32
 BANK = 512
 HALF = 256
+LIST_ROWS = 16
+
+PLACE = (0, 2, 1, 3)
+
+REUSED = {
+    "picked1_2": 1, "picked2_0": 4, "picked2_1": 4, "fore2_0": 7,
+    "f2_1": 11, "picked2_2": 18, "c1_1": 21, "fore2_3": 22,
+    "picked1_3": 29, "a_0": 32, "picked2_3": 39,
+    "c1_2": 43, "c1_0": 50, "fore2_1": 51, "fore2_2": 55, "c1_3": 55,
+    "c2_1": 63, "a_2": 64, "g_0": 71,
+    "c2_0": 75, "c2_2": 75,
+}
 
 
 def tile_attend_nexttoken_one_mixed_kernel(
@@ -28,16 +41,21 @@ def tile_attend_nexttoken_one_mixed_kernel(
     nc = tc.nc
     with ExitStack() as ctx:
         keep = ctx.enter_context(tc.tile_pool(name="keep", bufs=1))
+        strip = ctx.enter_context(tc.tile_pool(name="strip", bufs=1))
         psum = ctx.enter_context(tc.psum_pool(name="psum", bufs=8))
 
-        def f32_tiles(name, width, count):
-            return [keep.tile([P, width], F32, name="%s%d" % (name, n)) for n in range(count)]
+        def fresh(kind, k, width):
+            name = "%s_%d" % (kind, k)
+            if name in REUSED:
+                return strip.tile([P, width], F32, name=name, offset=REUSED[name] * P * 4)
+            return keep.tile([P, width], F32, name=name)
 
-        cs_stage = keep.tile([P, 2, T], U8, name="cs_stage")
-        scale_rows = cache_scales[0].rearrange("(g f) t -> f g t", f=PACK)
+        scale_stage = keep.tile([P, 2, T], U8, name="scale_stage")
+        scale_rows = cache_scales[0].rearrange("(quad f) t -> f quad t", f=PACK)
         for u in range(2):
             nc.sync.dma_start(
-                out=cs_stage[64 * u : 64 * u + PACK].bitcast(I32), in_=scale_rows[:, 2 * u : 2 * u + 2, :].bitcast(I32)
+                out=scale_stage[64 * u : 64 * u + PACK].bitcast(I32),
+                in_=scale_rows[:, 2 * u : 2 * u + 2, :].bitcast(I32),
             )
         q_rows = query.rearrange("(p j) q -> p j q", j=PACK)
         q_raw = []
@@ -49,72 +67,73 @@ def tile_attend_nexttoken_one_mixed_kernel(
         nc.sync.dma_start(out=cache_codes[:].bitcast(I32), in_=cache_words[0].bitcast(I32))
         lists = {}
         for name, src in (("offs", offs), ("offs2", offs2), ("offs4", offs4), ("offs3", offs3), ("offs5", offs5)):
-            lists[name] = keep.tile([P, I // 16], U16, name=name + "_sb")
+            lists[name] = keep.tile([P, I // LIST_ROWS], U16, name=name + "_sb")
             nc.sync.dma_start(lists[name][:], src)
         factor = keep.tile([P, PACK], F32, name="factor")
-        nc.sync.dma_start(out=factor[:], in_=rowf.rearrange("(p r) o -> p (r o)", r=PACK))
+        nc.sync.dma_start(out=factor[:], in_=rowf.rearrange("(p t) o -> p (t o)", t=PACK))
         mix_codes = keep.tile([P, PACK * E], U8, name="mix_codes", align_bytes=64)
         nc.sync.dma_start(
-            out=mix_codes[:].bitcast(I32), in_=mix_words[0].rearrange("p e r -> p (e r)").bitcast(I32)
+            out=mix_codes[:].bitcast(I32), in_=mix_words[0].rearrange("p e t -> p (e t)").bitcast(I32)
         )
 
         cache_plane = keep.tile([P, T], U8, name="cache_plane", align_bytes=64)
         nc.vector.memset(cache_plane[:].bitcast(I32), 0)
         mix_plane = keep.tile([P, E], U8, name="mix_plane", align_bytes=64)
         nc.gpsimd.memset(mix_plane[:].bitcast(I32), 0)
-        for g in range(PACK):
+        for quad in range(PACK):
             nc.sync.dma_start(
-                out=mix_plane[32 * g : 32 * g + PACK, :].bitcast(I32),
-                in_=mix_scales[0, PACK * g : PACK * (g + 1), :].bitcast(I32),
+                out=mix_plane[QUADRANT * quad : QUADRANT * quad + PACK, :].bitcast(I32),
+                in_=mix_scales[0, PACK * quad : PACK * (quad + 1), :].bitcast(I32),
             )
 
-        f1 = f32_tiles("f1_", T, 2)
-        f1 = [f1[0], f1[1], f1[0], f1[0]]
-        f2_even = keep.tile([P, T], F32, name="f2_even")
+        f1_first, f1_second = fresh("f1", 0, T), fresh("f1", 1, T)
+        f1 = [f1_first, f1_second, f1_first, f1_first]
+        f2_even = fresh("f2", 0, T)
         f2 = {0: f2_even, 2: f2_even}
         nc.vector.memset(f2_even[:], 0.0)
-        nc.vector.memset(f1[0][:], 0.0)
-        nc.gpsimd.memset(f1[1][:], 0.0)
-        a = [keep.tile([P, T], F32, name="a_%d" % r, tag="shared" if r == 0 else "a_%d" % r) for r in range(PACK)]
-        a1 = f32_tiles("a1_", T + 1, PACK)
-        nc.vector.memset(a1[0][:, 0:1], 0.0)
-        nc.vector.memset(a1[2][:, 0:1], 0.0)
-        for r in (1, 3):
-            nc.gpsimd.memset(a1[r][:, 0:1], 0.0)
+        nc.vector.memset(f1_first[:], 0.0)
+        nc.gpsimd.memset(f1_second[:], 0.0)
+        a = [fresh("a", k, T) for k in range(PACK)]
+        a1 = [fresh("a1", k, T + 1) for k in range(PACK)]
+        for k in (0, 2):
+            nc.vector.memset(a1[k][:, 0:1], 0.0)
+        for k in (1, 3):
+            nc.gpsimd.memset(a1[k][:, 0:1], 0.0)
 
-        for g in range(PACK):
+        for quad in range(PACK):
+            first_row = 64 * (quad // 2)
             nc.vector.tensor_copy(
-                out=cache_plane[32 * g : 32 * g + PACK, :].bitcast(I32), in_=cs_stage[64 * (g // 2) : 64 * (g // 2) + PACK, g % 2, :].bitcast(I32)
+                out=cache_plane[QUADRANT * quad : QUADRANT * quad + PACK, :].bitcast(I32),
+                in_=scale_stage[first_row : first_row + PACK, quad % 2, :].bitcast(I32),
             )
 
         q_first = keep.tile([P, P, PACK], BF16, name="q_first", align_bytes=64)
         q_rest = keep.tile([P, PACK - 1, P, PACK], BF16, name="q_rest", align_bytes=64)
+        dealt = [raw[:].rearrange("p j (s t) -> p s j t", t=PACK) for raw in q_raw]
+        columns = [slice(h * P // 2, (h + 1) * P // 2) for h in range(2)]
         for h in range(2):
-            s_range = slice(h * 64, (h + 1) * 64)
-            dealt = q_raw[h][:].rearrange("p j (s r) -> p s j r", r=PACK)
-            nc.vector.tensor_copy(out=q_first[:, s_range, :], in_=dealt[:, :, :, 0])
+            nc.vector.tensor_copy(out=q_first[:, columns[h], :], in_=dealt[h][:, :, :, 0])
             nc.scalar.activation(
-                out=q_rest[:, 0:2, s_range, :].rearrange("p r s j -> p s r j"),
-                in_=dealt[:, :, :, 1:3].rearrange("p s j r -> p s r j"),
+                out=q_rest[:, 0:2, columns[h], :].rearrange("p t s j -> p s t j"),
+                in_=dealt[h][:, :, :, 1:3].rearrange("p s j t -> p s t j"),
                 func=COPY,
             )
-        qc_first = keep.tile([P, P], U32, name="qc_first", align_bytes=64)
-        qs_first = keep.tile([P, P], U8, name="qs_first", align_bytes=64)
+        q_first_codes = keep.tile([P, P], U32, name="q_first_codes", align_bytes=64)
+        q_first_plane = keep.tile([P, P], U8, name="q_first_plane", align_bytes=64)
         nc.vector.quantize_mx(
-            out=qc_first[:].bitcast(FP8X4), scales=qs_first[:], in_=q_first[:].rearrange("p s j -> p (s j)")
+            out=q_first_codes[:].bitcast(FP8X4), scales=q_first_plane[:], in_=q_first[:].rearrange("p s j -> p (s j)")
         )
         for h in range(2):
-            dealt = q_raw[h][:].rearrange("p j (s r) -> p s j r", r=PACK)
-            nc.vector.tensor_copy(out=q_rest[:, 2, h * 64 : (h + 1) * 64, :], in_=dealt[:, :, :, 3])
-        qc_rest = keep.tile([P, 3 * P], U32, name="qc_rest", align_bytes=64)
-        qs_rest = keep.tile([P, 3 * P], U8, name="qs_rest", align_bytes=64)
+            nc.vector.tensor_copy(out=q_rest[:, 2, columns[h], :], in_=dealt[h][:, :, :, 3])
+        q_rest_codes = keep.tile([P, (PACK - 1) * P], U32, name="q_rest_codes", align_bytes=64)
+        q_rest_plane = keep.tile([P, (PACK - 1) * P], U8, name="q_rest_plane", align_bytes=64)
 
-        def scores(r, width):
-            if r == 0:
-                codes, plane = qc_first[:], qs_first[:]
+        def scores(k, width):
+            if k == 0:
+                codes, plane = q_first_codes[:], q_first_plane[:]
             else:
-                cols = slice((r - 1) * P, r * P)
-                codes, plane = qc_rest[:, cols], qs_rest[:, cols]
+                own = slice((PLACE[k] - 1) * P, PLACE[k] * P)
+                codes, plane = q_rest_codes[:, own], q_rest_plane[:, own]
             banks = []
             for b in range(T // width):
                 bank = psum.tile([P, BANK], F32, name="bank", tag="bank")
@@ -130,137 +149,151 @@ def tile_attend_nexttoken_one_mixed_kernel(
                 banks.append(bank[:, 0:width])
             return banks
 
-        strip = keep.tile([P, 23 * P], F32, name="strip")
-
-        def piece(start, width):
-            return strip[:, start * P : start * P + width]
-
-        own = f32_tiles("own_", I, 2)
-        c1_own = f32_tiles("c1_", T, 2)
-        w = f32_tiles("w_", I, PACK)
-        c1 = [piece(0, T), c1_own[0][:], piece(15, T), c1_own[1][:]]
-        picked2 = [piece(7, I), piece(7, I), piece(10, I), piece(12, I)]
-        picked1 = [own[0][:], own[1][:], own[0][:], piece(8, I)]
-        fore2 = [w[0][:], piece(0, I), piece(4, I), picked1[3]]
-        g = f32_tiles("g_", I, PACK)
-        c2 = f32_tiles("c2_", T, PACK)
+        w = [fresh("w", k, I) for k in range(PACK)]
+        picked1, picked2, fore2, c1, c2, g = {}, {}, {}, {}, {}, {}
         gw = keep.tile([P, I, PACK], BF16, name="gw", align_bytes=64)
 
-        def unload(r, banks, first_copy, second_copy):
+        def unload(k, banks, even_copy, odd_copy):
             width = T // len(banks)
             for b, bank in enumerate(banks):
-                (first_copy, second_copy)[b % 2](out=a1[r][:, 1 + b * width : 1 + (b + 1) * width], in_=bank)
-            nc.sync.dma_start(out=a[r][:], in_=a1[r][:, 1 : T + 1])
+                (even_copy, odd_copy)[b % 2](out=a1[k][:, 1 + b * width : 1 + (b + 1) * width], in_=bank)
+            nc.sync.dma_start(out=a[k][:], in_=a1[k][:, 1 : T + 1])
 
-        def pick_fore(r):
-            nc.vector.tensor_copy(out=picked1[r], in_=a1[r][:].indirect(lists["offs"][:]))
+        def pick_fore(k):
+            picked1[k] = fresh("picked1", k, I)
+            nc.vector.tensor_copy(out=picked1[k][:], in_=a1[k][:].indirect(lists["offs"][:]))
 
-        def pick_fore2(r):
-            nc.vector.tensor_copy(out=fore2[r], in_=a1[r][:].indirect(lists["offs2"][:]))
+        def pick_fore2(k):
+            fore2[k] = fresh("fore2", k, I)
+            nc.vector.tensor_copy(out=fore2[k][:], in_=a1[k][:].indirect(lists["offs2"][:]))
 
-        def pick_score2(r):
-            nc.vector.tensor_copy(out=picked2[r], in_=a[r][:].indirect(lists["offs2"][:]))
+        def pick_score2(k):
+            picked2[k] = fresh("picked2", k, I)
+            nc.vector.tensor_copy(out=picked2[k][:], in_=a[k][:].indirect(lists["offs2"][:]))
 
-        def larger(r):
-            nc.vector.tensor_tensor(out=w[r][:], in0=picked1[r], in1=picked2[r], op=ALU.max)
+        def make_w(k):
+            nc.vector.tensor_tensor(out=w[k][:], in0=picked1[k][:], in1=picked2[k][:], op=ALU.max)
 
-        def put_f1(r):
-            nc.scalar.activation(out=f1[r][:].indirect(lists["offs3"][:]), in_=w[r][:], func=COPY)
+        def put_f1(k):
+            nc.scalar.activation(out=f1[k][:].indirect(lists["offs3"][:]), in_=w[k][:], func=COPY)
 
-        def put_f2(r):
-            nc.scalar.activation(out=f2[r][:].indirect(lists["offs4"][:]), in_=picked1[r], func=COPY)
+        def put_f2(k):
+            nc.scalar.activation(out=f2[k][:].indirect(lists["offs4"][:]), in_=picked1[k][:], func=COPY)
 
-        def make_c1(r, engine):
-            engine.tensor_tensor(out=c1[r], in0=a[r][:], in1=f1[r][:], op=ALU.subtract)
+        def make_c1(k, engine, lo, hi):
+            if lo == 0:
+                c1[k] = fresh("c1", k, T)
+            engine.tensor_tensor(out=c1[k][:, lo:hi], in0=a[k][:, lo:hi], in1=f1[k][:, lo:hi], op=ALU.subtract)
 
-        def make_c2(r):
-            nc.vector.tensor_tensor(out=c2[r][:], in0=c1[r], in1=f2[r][:], op=ALU.max)
+        def make_c2(k):
+            c2[k] = fresh("c2", k, T)
+            nc.vector.tensor_tensor(out=c2[k][:], in0=c1[k][:], in1=f2[k][:], op=ALU.max)
 
-        def result(r, lo, hi):
+        def make_g(k, lo, hi):
+            if lo == 0:
+                g[k] = fresh("g", k, I)
             nc.vector.tensor_tensor(
-                out=g[r][:, lo:hi],
-                in0=c2[r][:].indirect(lists["offs5"][:, lo // 16 : hi // 16]),
-                in1=fore2[r][:, lo:hi],
+                out=g[k][:, lo:hi],
+                in0=c2[k][:].indirect(lists["offs5"][:, lo // LIST_ROWS : hi // LIST_ROWS]),
+                in1=fore2[k][:, lo:hi],
                 op=ALU.add,
             )
 
-        def weigh(r, lo, hi):
+        def weigh(k, lo, hi):
+            t = PLACE[k]
             nc.vector.tensor_scalar(
-                out=gw[:, lo:hi, r], in0=g[r][:, lo:hi], scalar1=factor[:, r : r + 1], scalar2=None, op0=ALU.mult
+                out=gw[:, lo:hi, t], in0=g[k][:, lo:hi], scalar1=factor[:, t : t + 1], scalar2=None, op0=ALU.mult
             )
 
-        banks0 = scores(0, HALF)
+        def weigh_on_scalar(k, lo, hi):
+            t = PLACE[k]
+            nc.scalar.activation(out=gw[:, lo:hi, t], in_=g[k][:, lo:hi], func=COPY, scale=factor[:, t : t + 1])
+
+        banks_first = scores(0, HALF)
         nc.vector.quantize_mx(
-            out=qc_rest[:].bitcast(FP8X4), scales=qs_rest[:], in_=q_rest[:].rearrange("p r s j -> p (r s j)")
+            out=q_rest_codes[:].bitcast(FP8X4),
+            scales=q_rest_plane[:],
+            in_=q_rest[:].rearrange("p t s j -> p (t s j)"),
         )
-        unload(0, banks0, nc.vector.tensor_copy, nc.scalar.copy)
-        later = [None] + [scores(r, BANK) for r in range(1, PACK)]
+        unload(0, banks_first, nc.vector.tensor_copy, nc.scalar.copy)
+        banks_later = {k: scores(k, BANK) for k in range(1, PACK)}
+
         pick_fore(0)
-        unload(1, later[1], nc.scalar.copy, nc.scalar.copy)
+        unload(1, banks_later[1], nc.scalar.copy, nc.scalar.copy)
         put_f2(0)
         pick_fore(1)
         pick_score2(0)
-        larger(0)
-        unload(2, later[2], nc.vector.tensor_copy, nc.vector.tensor_copy)
-        unload(3, later[3], nc.scalar.copy, nc.scalar.copy)
+        make_w(0)
+        unload(2, banks_later[2], nc.vector.tensor_copy, nc.vector.tensor_copy)
+        unload(3, banks_later[3], nc.scalar.copy, nc.scalar.copy)
         put_f1(0)
         pick_score2(1)
-        pick_fore(2)
-        larger(1)
+        make_w(1)
         put_f1(1)
-        make_c1(0, nc.gpsimd)
-        f2_odd = keep.tile([P, T], F32, name="f2_odd", tag="shared")
+
+        make_c1(0, nc.gpsimd, 0, T)
+        pick_fore(2)
+        pick_score2(2)
+        pick_fore2(0)
+        make_w(2)
+        put_f1(2)
+
+        f2_odd = fresh("f2", 1, T)
         nc.gpsimd.memset(f2_odd[:], 0.0)
         f2[1] = f2_odd
         f2[3] = f2_odd
-        pick_score2(2)
-        pick_fore2(0)
-        larger(2)
-        put_f1(2)
-        make_c1(1, nc.gpsimd)
+        make_c1(1, nc.gpsimd, 0, T // 2)
         put_f2(1)
         pick_score2(3)
         pick_fore(3)
+        make_c1(1, nc.vector, T // 2, T)
         make_c2(0)
-        larger(3)
+        make_w(3)
         put_f2(2)
-        make_c1(2, nc.gpsimd)
+
+        make_c1(2, nc.gpsimd, 0, T)
         put_f1(3)
         pick_fore2(1)
         pick_fore2(2)
-        result(0, 0, I)
+
         make_c2(1)
         put_f2(3)
-        weigh(0, 0, I)
-        result(1, 0, I)
+        make_g(0, 0, I)
+        make_g(1, 0, I)
         make_c2(2)
+        weigh(0, HALF, I)
+        make_g(2, 0, I)
+        make_c1(3, nc.vector, 0, T)
         weigh(1, 0, I)
-        result(2, 0, I)
-        make_c1(3, nc.vector)
-        weigh(2, 0, I)
-        nc.scalar.activation(out=fore2[3], in_=a1[3][:].indirect(lists["offs2"][:]), func=COPY)
+
+        fore2[3] = fresh("fore2", 3, I)
+        nc.scalar.activation(out=fore2[3][:], in_=a1[3][:].indirect(lists["offs2"][:]), func=COPY)
+        weigh_on_scalar(0, 0, HALF)
+        weigh_on_scalar(2, 0, HALF)
+        weigh_on_scalar(2, HALF, I)
         make_c2(3)
         for h in range(2):
-            result(3, h * HALF, (h + 1) * HALF)
+            make_g(3, h * HALF, (h + 1) * HALF)
         for h in range(2):
             weigh(3, h * HALF, (h + 1) * HALF)
 
         out_rows = out.rearrange("(b p) i -> p b i", p=P)
         for h in range(2):
-            gc = keep.tile([P, HALF], U32, name="gc%d" % h, align_bytes=64)
-            gs = keep.tile([P, HALF], U8, name="gs%d" % h, align_bytes=64)
+            slots = slice(h * HALF, (h + 1) * HALF)
+            gw_codes = keep.tile([P, HALF], U32, name="gw_codes%d" % h, align_bytes=64)
+            gw_plane = keep.tile([P, HALF], U8, name="gw_plane%d" % h, align_bytes=64)
             nc.vector.quantize_mx(
-                out=gc[:].bitcast(FP8X4), scales=gs[:], in_=gw[:, h * HALF : (h + 1) * HALF, :].rearrange("p i r -> p (i r)")
+                out=gw_codes[:].bitcast(FP8X4), scales=gw_plane[:], in_=gw[:, slots, :].rearrange("p i t -> p (i t)")
             )
-            staged = keep.tile([P, 2, HALF], F32, name="staged%d" % h)
-            for b in range(2):
+            staged = keep.tile([P, E // P, HALF], F32, name="staged%d" % h)
+            for b in range(E // P):
                 bank = psum.tile([P, BANK], F32, name="bank", tag="bank")
                 nc.tensor.matmul_mx(
                     out=bank[:, 0:HALF],
                     lhsT=mix_codes[:, PACK * P * b : PACK * P * (b + 1)].bitcast(FP8X4),
                     lhsT_scale=mix_plane[:, P * b : P * (b + 1)],
-                    rhs=gc[:].bitcast(FP8X4),
-                    rhs_scale=gs[:],
+                    rhs=gw_codes[:].bitcast(FP8X4),
+                    rhs_scale=gw_plane[:],
                     start=True,
                     stop=True,
                 )
@@ -269,7 +302,7 @@ def tile_attend_nexttoken_one_mixed_kernel(
                 else:
                     nc.scalar.copy(out=staged[:, b, :], in_=bank[:, 0:HALF])
             if h == 0:
-                nc.sync.dma_start(out=out_rows[:, :, 0:HALF], in_=staged[:])
+                nc.sync.dma_start(out=out_rows[:, :, slots], in_=staged[:])
             else:
-                nc.sync.dma_start(out=out_rows[:, 0, HALF:I], in_=staged[:, 0, :])
-                nc.scalar.dma_start(out=out_rows[:, 1, HALF:I], in_=staged[:, 1, :])
+                nc.sync.dma_start(out=out_rows[:, 0, slots], in_=staged[:, 0, :])
+                nc.scalar.dma_start(out=out_rows[:, 1, slots], in_=staged[:, 1, :])

from contextlib import ExitStack

import concourse.mybir as mybir

D, T, I, Q, E = 512, 1024, 512, 512, 256
FLOPS = 2 * D * Q * T + 2 * Q * E * I

F32 = mybir.dt.float32
BF16 = mybir.dt.bfloat16
I32 = mybir.dt.int32
U32 = mybir.dt.uint32
U16 = mybir.dt.uint16
U8 = mybir.dt.uint8
FP8X4 = mybir.dt.float8_e4m3fn_x4
FP4X4 = mybir.dt.float4_e2m1fn_x4
ALU = mybir.AluOpType
COPY = mybir.ActivationFunctionType.Copy

P = 128
PACK = 4
QUADRANT = 32
BANK = 512
HALF = 256
LIST_ROWS = 16

PLACE = (0, 2, 1, 3)

REUSED = {
    "picked1_2": 1, "picked2_0": 4, "picked2_1": 4, "fore2_0": 7,
    "f2_1": 11, "picked2_2": 18, "c1_1": 21, "fore2_3": 22,
    "picked1_3": 29, "a_0": 32, "picked2_3": 39,
    "c1_2": 43, "c1_0": 50, "fore2_1": 51, "fore2_2": 55, "c1_3": 55,
    "c2_1": 63, "a_2": 64, "g_0": 71,
    "c2_0": 75, "c2_2": 75,
}


def tile_attend_nexttoken_one_mixed_kernel(
    tc, query, cache_words, cache_scales, rowf, mix_words, mix_scales, offs, offs2, offs3, offs4, offs5, out
):
    nc = tc.nc
    with ExitStack() as ctx:
        keep = ctx.enter_context(tc.tile_pool(name="keep", bufs=1))
        strip = ctx.enter_context(tc.tile_pool(name="strip", bufs=1))
        psum = ctx.enter_context(tc.psum_pool(name="psum", bufs=8))

        def fresh(kind, k, width):
            name = "%s_%d" % (kind, k)
            if name in REUSED:
                return strip.tile([P, width], F32, name=name, offset=REUSED[name] * P * 4)
            return keep.tile([P, width], F32, name=name)

        scale_stage = keep.tile([P, 2, T], U8, name="scale_stage")
        scale_rows = cache_scales[0].rearrange("(quad f) t -> f quad t", f=PACK)
        for u in range(2):
            nc.sync.dma_start(
                out=scale_stage[64 * u : 64 * u + PACK].bitcast(I32),
                in_=scale_rows[:, 2 * u : 2 * u + 2, :].bitcast(I32),
            )
        q_rows = query.rearrange("(p j) q -> p j q", j=PACK)
        q_raw = []
        for h in range(2):
            raw = keep.tile([P, PACK, HALF], F32, name="q_raw%d" % h)
            nc.sync.dma_start(out=raw[:], in_=q_rows[:, :, h * HALF : (h + 1) * HALF])
            q_raw.append(raw)
        cache_codes = keep.tile([P, 2 * T], U8, name="cache_codes", align_bytes=64)
        nc.sync.dma_start(out=cache_codes[:].bitcast(I32), in_=cache_words[0].bitcast(I32))
        lists = {}
        for name, src in (("offs", offs), ("offs2", offs2), ("offs4", offs4), ("offs3", offs3), ("offs5", offs5)):
            lists[name] = keep.tile([P, I // LIST_ROWS], U16, name=name + "_sb")
            nc.sync.dma_start(lists[name][:], src)
        factor = keep.tile([P, PACK], F32, name="factor")
        nc.sync.dma_start(out=factor[:], in_=rowf.rearrange("(p t) o -> p (t o)", t=PACK))
        mix_codes = keep.tile([P, PACK * E], U8, name="mix_codes", align_bytes=64)
        nc.sync.dma_start(
            out=mix_codes[:].bitcast(I32), in_=mix_words[0].rearrange("p e t -> p (e t)").bitcast(I32)
        )

        cache_plane = keep.tile([P, T], U8, name="cache_plane", align_bytes=64)
        nc.vector.memset(cache_plane[:].bitcast(I32), 0)
        mix_plane = keep.tile([P, E], U8, name="mix_plane", align_bytes=64)
        nc.gpsimd.memset(mix_plane[:].bitcast(I32), 0)
        for quad in range(PACK):
            nc.sync.dma_start(
                out=mix_plane[QUADRANT * quad : QUADRANT * quad + PACK, :].bitcast(I32),
                in_=mix_scales[0, PACK * quad : PACK * (quad + 1), :].bitcast(I32),
            )

        f1_first, f1_second = fresh("f1", 0, T), fresh("f1", 1, T)
        f1 = [f1_first, f1_second, f1_first, f1_first]
        f2_even = fresh("f2", 0, T)
        f2 = {0: f2_even, 2: f2_even}
        nc.vector.memset(f2_even[:], 0.0)
        nc.vector.memset(f1_first[:], 0.0)
        nc.gpsimd.memset(f1_second[:], 0.0)
        a = [fresh("a", k, T) for k in range(PACK)]
        a1 = [fresh("a1", k, T + 1) for k in range(PACK)]
        for k in (0, 2):
            nc.vector.memset(a1[k][:, 0:1], 0.0)
        for k in (1, 3):
            nc.gpsimd.memset(a1[k][:, 0:1], 0.0)

        for quad in range(PACK):
            first_row = 64 * (quad // 2)
            nc.vector.tensor_copy(
                out=cache_plane[QUADRANT * quad : QUADRANT * quad + PACK, :].bitcast(I32),
                in_=scale_stage[first_row : first_row + PACK, quad % 2, :].bitcast(I32),
            )

        q_first = keep.tile([P, P, PACK], BF16, name="q_first", align_bytes=64)
        q_rest = keep.tile([P, PACK - 1, P, PACK], BF16, name="q_rest", align_bytes=64)
        dealt = [raw[:].rearrange("p j (s t) -> p s j t", t=PACK) for raw in q_raw]
        columns = [slice(h * P // 2, (h + 1) * P // 2) for h in range(2)]
        for h in range(2):
            nc.vector.tensor_copy(out=q_first[:, columns[h], :], in_=dealt[h][:, :, :, 0])
            nc.scalar.activation(
                out=q_rest[:, 0:2, columns[h], :].rearrange("p t s j -> p s t j"),
                in_=dealt[h][:, :, :, 1:3].rearrange("p s j t -> p s t j"),
                func=COPY,
            )
        q_first_codes = keep.tile([P, P], U32, name="q_first_codes", align_bytes=64)
        q_first_plane = keep.tile([P, P], U8, name="q_first_plane", align_bytes=64)
        nc.vector.quantize_mx(
            out=q_first_codes[:].bitcast(FP8X4), scales=q_first_plane[:], in_=q_first[:].rearrange("p s j -> p (s j)")
        )
        for h in range(2):
            nc.vector.tensor_copy(out=q_rest[:, 2, columns[h], :], in_=dealt[h][:, :, :, 3])
        q_rest_codes = keep.tile([P, (PACK - 1) * P], U32, name="q_rest_codes", align_bytes=64)
        q_rest_plane = keep.tile([P, (PACK - 1) * P], U8, name="q_rest_plane", align_bytes=64)

        def scores(k, width):
            if k == 0:
                codes, plane = q_first_codes[:], q_first_plane[:]
            else:
                own = slice((PLACE[k] - 1) * P, PLACE[k] * P)
                codes, plane = q_rest_codes[:, own], q_rest_plane[:, own]
            banks = []
            for b in range(T // width):
                bank = psum.tile([P, BANK], F32, name="bank", tag="bank")
                nc.tensor.matmul_mx(
                    out=bank[:, 0:width],
                    lhsT=codes.bitcast(FP8X4),
                    lhsT_scale=plane,
                    rhs=cache_codes[:, 2 * width * b : 2 * width * (b + 1)].bitcast(FP4X4),
                    rhs_scale=cache_plane[:, width * b : width * (b + 1)],
                    start=True,
                    stop=True,
                )
                banks.append(bank[:, 0:width])
            return banks

        w = [fresh("w", k, I) for k in range(PACK)]
        picked1, picked2, fore2, c1, c2, g = {}, {}, {}, {}, {}, {}
        gw = keep.tile([P, I, PACK], BF16, name="gw", align_bytes=64)

        def unload(k, banks, even_copy, odd_copy):
            width = T // len(banks)
            for b, bank in enumerate(banks):
                (even_copy, odd_copy)[b % 2](out=a1[k][:, 1 + b * width : 1 + (b + 1) * width], in_=bank)
            nc.sync.dma_start(out=a[k][:], in_=a1[k][:, 1 : T + 1])

        def pick_fore(k):
            picked1[k] = fresh("picked1", k, I)
            nc.vector.tensor_copy(out=picked1[k][:], in_=a1[k][:].indirect(lists["offs"][:]))

        def pick_fore2(k):
            fore2[k] = fresh("fore2", k, I)
            nc.vector.tensor_copy(out=fore2[k][:], in_=a1[k][:].indirect(lists["offs2"][:]))

        def pick_score2(k):
            picked2[k] = fresh("picked2", k, I)
            nc.vector.tensor_copy(out=picked2[k][:], in_=a[k][:].indirect(lists["offs2"][:]))

        def make_w(k):
            nc.vector.tensor_tensor(out=w[k][:], in0=picked1[k][:], in1=picked2[k][:], op=ALU.max)

        def put_f1(k):
            nc.scalar.activation(out=f1[k][:].indirect(lists["offs3"][:]), in_=w[k][:], func=COPY)

        def put_f2(k):
            nc.scalar.activation(out=f2[k][:].indirect(lists["offs4"][:]), in_=picked1[k][:], func=COPY)

        def make_c1(k, engine, lo, hi):
            if lo == 0:
                c1[k] = fresh("c1", k, T)
            engine.tensor_tensor(out=c1[k][:, lo:hi], in0=a[k][:, lo:hi], in1=f1[k][:, lo:hi], op=ALU.subtract)

        def make_c2(k):
            c2[k] = fresh("c2", k, T)
            nc.vector.tensor_tensor(out=c2[k][:], in0=c1[k][:], in1=f2[k][:], op=ALU.max)

        def make_g(k, lo, hi):
            if lo == 0:
                g[k] = fresh("g", k, I)
            nc.vector.tensor_tensor(
                out=g[k][:, lo:hi],
                in0=c2[k][:].indirect(lists["offs5"][:, lo // LIST_ROWS : hi // LIST_ROWS]),
                in1=fore2[k][:, lo:hi],
                op=ALU.add,
            )

        def weigh(k, lo, hi):
            t = PLACE[k]
            nc.vector.tensor_scalar(
                out=gw[:, lo:hi, t], in0=g[k][:, lo:hi], scalar1=factor[:, t : t + 1], scalar2=None, op0=ALU.mult
            )

        def weigh_on_scalar(k, lo, hi):
            t = PLACE[k]
            nc.scalar.activation(out=gw[:, lo:hi, t], in_=g[k][:, lo:hi], func=COPY, scale=factor[:, t : t + 1])

        banks_first = scores(0, HALF)
        nc.vector.quantize_mx(
            out=q_rest_codes[:].bitcast(FP8X4),
            scales=q_rest_plane[:],
            in_=q_rest[:].rearrange("p t s j -> p (t s j)"),
        )
        unload(0, banks_first, nc.vector.tensor_copy, nc.scalar.copy)
        banks_later = {k: scores(k, BANK) for k in range(1, PACK)}

        pick_fore(0)
        unload(1, banks_later[1], nc.scalar.copy, nc.scalar.copy)
        put_f2(0)
        pick_fore(1)
        pick_score2(0)
        make_w(0)
        unload(2, banks_later[2], nc.vector.tensor_copy, nc.vector.tensor_copy)
        unload(3, banks_later[3], nc.scalar.copy, nc.scalar.copy)
        put_f1(0)
        pick_score2(1)
        make_w(1)
        put_f1(1)

        make_c1(0, nc.gpsimd, 0, T)
        pick_fore(2)
        pick_score2(2)
        pick_fore2(0)
        make_w(2)
        put_f1(2)

        f2_odd = fresh("f2", 1, T)
        nc.gpsimd.memset(f2_odd[:], 0.0)
        f2[1] = f2_odd
        f2[3] = f2_odd
        make_c1(1, nc.gpsimd, 0, T // 2)
        put_f2(1)
        pick_score2(3)
        pick_fore(3)
        make_c1(1, nc.vector, T // 2, T)
        make_c2(0)
        make_w(3)
        put_f2(2)

        make_c1(2, nc.gpsimd, 0, T)
        put_f1(3)
        pick_fore2(1)
        pick_fore2(2)

        make_c2(1)
        put_f2(3)
        make_g(0, 0, I)
        make_g(1, 0, I)
        make_c2(2)
        weigh(0, HALF, I)
        make_g(2, 0, I)
        make_c1(3, nc.vector, 0, T)
        weigh(1, 0, I)

        fore2[3] = fresh("fore2", 3, I)
        nc.scalar.activation(out=fore2[3][:], in_=a1[3][:].indirect(lists["offs2"][:]), func=COPY)
        weigh_on_scalar(0, 0, HALF)
        weigh_on_scalar(2, 0, HALF)
        weigh_on_scalar(2, HALF, I)
        make_c2(3)
        for h in range(2):
            make_g(3, h * HALF, (h + 1) * HALF)
        for h in range(2):
            weigh(3, h * HALF, (h + 1) * HALF)

        out_rows = out.rearrange("(b p) i -> p b i", p=P)
        for h in range(2):
            slots = slice(h * HALF, (h + 1) * HALF)
            gw_codes = keep.tile([P, HALF], U32, name="gw_codes%d" % h, align_bytes=64)
            gw_plane = keep.tile([P, HALF], U8, name="gw_plane%d" % h, align_bytes=64)
            nc.vector.quantize_mx(
                out=gw_codes[:].bitcast(FP8X4), scales=gw_plane[:], in_=gw[:, slots, :].rearrange("p i t -> p (i t)")
            )
            staged = keep.tile([P, E // P, HALF], F32, name="staged%d" % h)
            for b in range(E // P):
                bank = psum.tile([P, BANK], F32, name="bank", tag="bank")
                nc.tensor.matmul_mx(
                    out=bank[:, 0:HALF],
                    lhsT=mix_codes[:, PACK * P * b : PACK * P * (b + 1)].bitcast(FP8X4),
                    lhsT_scale=mix_plane[:, P * b : P * (b + 1)],
                    rhs=gw_codes[:].bitcast(FP8X4),
                    rhs_scale=gw_plane[:],
                    start=True,
                    stop=True,
                )
                if h == 1 and b == 0:
                    nc.vector.tensor_copy(out=staged[:, b, :], in_=bank[:, 0:HALF])
                else:
                    nc.scalar.copy(out=staged[:, b, :], in_=bank[:, 0:HALF])
            if h == 0:
                nc.sync.dma_start(out=out_rows[:, :, slots], in_=staged[:])
            else:
                nc.sync.dma_start(out=out_rows[:, 0, slots], in_=staged[:, 0, :])
                nc.scalar.dma_start(out=out_rows[:, 1, slots], in_=staged[:, 1, :])
